import numpy as np
import ml_dtypes


def mxq(x, axis, fmt="e4m3"):
    dtype, down = {"e4m3": (ml_dtypes.float8_e4m3fn, 7), "e5m2": (ml_dtypes.float8_e5m2, 14)}[fmt]
    v = np.moveaxis(np.asarray(x, np.float32).astype(ml_dtypes.bfloat16).astype(np.float64), axis, -1)
    blocks = v.reshape(v.shape[:-1] + (-1, 32))
    amax = np.abs(blocks).max(-1, keepdims=True)
    byte = np.maximum(np.where(amax > 0, np.frexp(amax)[1] - 1 + 127, 0) - down, 1)
    scale = np.exp2(byte - 127.0)
    codes = (blocks / scale).astype(np.float32).astype(dtype).astype(np.float64)
    return np.moveaxis((codes * scale).reshape(v.shape), -1, axis)


WIDE = False


def mx_kscale(k):
    if not WIDE:
        return np.ones(k)
    levels = np.array([30, -30])
    if k % 512:
        return np.exp2(np.random.permutation(np.resize(levels, k // 32))).repeat(32)
    a = np.empty((k // 512, 16))
    for p in range(k // 512):
        a[p, :8] = np.random.permutation(np.resize(levels, 8))
        for g in range(8):
            far = levels[np.abs(levels - a[p, g]) >= 10]
            a[p, g + 8] = far[np.random.randint(len(far))]
    return np.exp2(a.ravel()).repeat(32)


def f64(x):
    return np.asarray(x).astype(np.float64)


def planes(y):
    n, m = y.shape
    v = y.astype(np.float32).astype(ml_dtypes.bfloat16).astype(np.float64).reshape(n // 32, 32, m)
    top = np.abs(v).max(1)
    byte = np.clip(np.where(top > 0, np.frexp(top)[1] - 1 + 127 - 7, 1), 1, 254)
    codes = (v * np.exp2(127.0 - byte)[:, None, :]).reshape(n, m).astype(np.float32).astype(ml_dtypes.float8_e4m3fn).view(np.uint8)
    words = codes.reshape(n // 512, 128, 4, m).transpose(0, 1, 3, 2)
    return np.ascontiguousarray(words), np.ascontiguousarray(byte.astype(np.uint8).reshape(n // 512, 16, m))


K, M, T = 2048, 512, 512


def setup_inputs():
    n = np.random.standard_normal
    s1 = mx_kscale(K)[:, None]
    s2 = mx_kscale(K)[:, None]
    return {
        "w": (n((K, M)) / np.sqrt(K) * s1).astype(np.float32),
        "xd": (n((K, T)) / s1).astype(np.float32),
        "wd": (n((K, M)) / np.sqrt(K) * s2).astype(np.float32),
        "x": (n((K, T)) / s2).astype(np.float32),
    }


def reference(w, xd, wd, x):
    w_ = mxq(f64(w), 0, "e4m3")
    xd_ = mxq(f64(xd), 0, "e5m2")
    wd_ = mxq(f64(wd), 0, "e5m2")
    x_ = mxq(f64(x), 0, "e4m3")
    y = xd_.T @ w_ + x_.T @ wd_
    out_0 = y
    return (out_0,) + planes(out_0)

@@ -1,0 +1,191 @@
+from contextlib import ExitStack
+
+import concourse.mybir as mybir
+
+K, M, T = 2048, 512, 512
+FLOPS = 2 * 2 * K * M * T
+
+F32 = mybir.dt.float32
+BF16 = mybir.dt.bfloat16
+I32 = mybir.dt.int32
+U32 = mybir.dt.uint32
+U8 = mybir.dt.uint8
+E4M3 = mybir.dt.float8_e4m3fn_x4
+E5M2 = mybir.dt.float8_e5m2_x4
+
+P = 128
+PACK = 4
+K_PASS = P * PACK
+PASSES = K // K_PASS
+HALF = M // 2
+
+
+def tile_mix_jvp_tm_pl_none_kernel(tc, w, xd, wd, x, out_0, out_1, out_2):
+    nc = tc.nc
+    with ExitStack() as ctx:
+        keep = ctx.enter_context(tc.tile_pool(name="keep", bufs=1))
+        stage = ctx.enter_context(tc.tile_pool(name="stage", bufs=4))
+        psum = ctx.enter_context(tc.psum_pool(name="psum", bufs=1))
+        ctx.enter_context(tc.manual_schedule())
+
+        def load_passes(name, src, g0, g1):
+            raw = keep.tile([P, g1 - g0, PACK, M], F32, name=name)
+            nc.sync.dma_start(
+                out=raw[:].rearrange("p g j n -> p g (j n)"),
+                in_=src[g0 * K_PASS : g1 * K_PASS, :].rearrange("(g p j) n -> p g (j n)", p=P, j=PACK),
+            )
+            return [raw[:, g, :, :] for g in range(g1 - g0)]
+
+        def load_half(name, src, g, h):
+            raw = keep.tile([P, PACK, HALF], F32, name=name)
+            nc.sync.dma_start(
+                out=raw[:],
+                in_=src[g * K_PASS : (g + 1) * K_PASS, h * HALF : (h + 1) * HALF].rearrange("(p j) n -> p j n", j=PACK),
+            )
+            return raw[:]
+
+        xd_raw = load_passes("xd_raw", xd, 0, 4)
+        w_raw = load_passes("w_raw01", w, 0, 2)
+        w_raw = w_raw + load_passes("w_raw23", w, 2, 4)
+        x_raw = load_passes("x_raw01", x, 0, 2)
+        wd_raw = load_passes("wd_raw0", wd, 0, 1)
+        wd_raw = wd_raw + load_passes("wd_raw1", wd, 1, 2)
+        late_raw = {}
+        for g in (2, 3):
+            x_raw = x_raw + load_passes("x_raw%d" % g, x, g, g + 1)
+            late_raw[g, 0] = load_half("wd_raw%d_0" % g, wd, g, 0)
+        for g in (2, 3):
+            late_raw[g, 1] = load_half("wd_raw%d_1" % g, wd, g, 1)
+
+        def mx_tiles(name, width):
+            codes = keep.tile([P, width], U32, name=name + "_codes", align_bytes=64)
+            scales = keep.tile([P, width], U8, name=name + "_scales", align_bytes=64)
+            return codes, scales
+
+        xd_q = [mx_tiles("xd%d" % g, T) for g in range(PASSES)]
+        w_q = [mx_tiles("w%d" % g, M) for g in range(PASSES)]
+        x_q = [mx_tiles("x%d" % g, T) for g in range(PASSES)]
+        wd_q = [mx_tiles("wd%d" % g, M) for g in range(2)]
+        late_q = {g: mx_tiles("wd%d" % g, 3 * HALF) for g in (2, 3)}
+        for g in (2, 3):
+            nc.vector.memset(late_q[g][0][:, HALF : 2 * HALF], 0)
+            nc.vector.memset(late_q[g][1][:, HALF : 2 * HALF].bitcast(U32), 0)
+
+        banks = [[psum.tile([P, M], F32, name="acc%d_%d" % (h, r)) for r in range(PACK)] for h in range(2)]
+        result = [keep.tile([P, PACK, HALF], F32, name="result%d" % h) for h in range(2)]
+        out_codes, out_scales = mx_tiles("out", M)
+
+        def new_grouped():
+            grouped = stage.tile([P, PACK * M], BF16, name="grouped", align_bytes=64)
+            return grouped
+
+        def interleave(copy, grouped, raw, c0, c1):
+            copy(
+                out=grouped[:, PACK * c0 : PACK * c1].rearrange("p (c i j) -> p c j i", i=4, j=PACK),
+                in_=raw[:, :, c0:c1].rearrange("p j (c i) -> p c j i", i=4),
+            )
+
+        def interleave_dealt(copy, grouped, raw, c0, c1):
+            copy(
+                out=grouped[:].rearrange("p (r m j) -> p m r j", r=PACK, j=PACK)[:, c0 // PACK : c1 // PACK, :, :],
+                in_=raw[:, :, c0:c1].rearrange("p j (m r) -> p m r j", r=PACK),
+            )
+
+        def cast(kind, raw, on_scalar):
+            grouped = new_grouped()
+            width = raw.shape[2]
+            kind(nc.scalar.copy, grouped, raw, 0, on_scalar)
+            kind(nc.vector.tensor_copy, grouped, raw, on_scalar, width)
+            return grouped[:, : PACK * width]
+
+        def quantize(grouped, codes, scales, fmt):
+            nc.vector.quantize_mx(out=codes.bitcast(fmt), scales=scales, in_=grouped)
+
+        def multiply(h, stat, stat_fmt, mov_codes, mov_scales, mov_fmt, start, stop, rs=range(PACK)):
+            for r in rs:
+                cols = slice(r * P, (r + 1) * P)
+                nc.tensor.matmul_mx(
+                    out=banks[h][r][:],
+                    lhsT=stat[0][:, cols].bitcast(stat_fmt),
+                    lhsT_scale=stat[1][:, cols],
+                    rhs=mov_codes.bitcast(mov_fmt),
+                    rhs_scale=mov_scales,
+                    start=start,
+                    stop=stop,
+                )
+
+        def run(kind, raws, quants, fmt, g0, g1, after):
+            pending = None
+            for g in range(g0, g1 + 1):
+                grouped = cast(kind, raws[g], 256) if g < g1 else None
+                if pending is not None:
+                    quantize(pending, quants[g - 1][0][:], quants[g - 1][1][:], fmt)
+                    after(g - 1)
+                pending = grouped
+
+        def first_product(g):
+            for h in range(2):
+                multiply(h, xd_q[g], E5M2, w_q[g][0][:], w_q[g][1][:], E4M3, g == 0, False)
+
+        def second_product(g, h, rs=range(PACK)):
+            multiply(h, x_q[g], E4M3, wd_q[g][0][:], wd_q[g][1][:], E5M2, False, False, rs)
+
+        def nothing(g):
+            return None
+
+        run(interleave_dealt, xd_raw, xd_q, E5M2, 0, 4, nothing)
+        run(interleave, w_raw, w_q, E4M3, 0, 2, first_product)
+        run(interleave, w_raw, w_q, E4M3, 2, 4, first_product)
+        run(interleave_dealt, x_raw, x_q, E4M3, 0, 2, nothing)
+        run(interleave, wd_raw, wd_q, E5M2, 0, 1, nothing)
+        second_product(0, 0)
+        second_product(0, 1)
+        run(interleave, wd_raw, wd_q, E5M2, 1, 2, nothing)
+        second_product(1, 0)
+        second_product(1, 1, (0, 1))
+
+        def late_quantize(g, h, grouped):
+            cols = slice(2 * h * HALF, (2 * h + 1) * HALF)
+            quantize(grouped, late_q[g][0][:, cols], late_q[g][1][:, cols], E5M2)
+            window = slice(h * HALF, h * HALF + M)
+            multiply(h, x_q[g], E4M3, late_q[g][0][:, window], late_q[g][1][:, window], E5M2, False, g == 3)
+
+        def drain(h, r):
+            nc.scalar.copy(out=result[h][:, r, :], in_=banks[h][r][:, h * HALF : (h + 1) * HALF])
+
+        def store_result(h, r0, r1):
+            nc.sync.dma_start(
+                out=out_0[:, h * HALF : (h + 1) * HALF].rearrange("(p r) n -> p r n", r=PACK)[:, r0:r1, :],
+                in_=result[h][:, r0:r1, :],
+            )
+
+        words = out_1[0].rearrange("p n i -> p (n i)").bitcast(I32)
+        scale_rows = out_2[0].bitcast(I32)
+
+        def quantize_result(h):
+            cols = slice(h * HALF, (h + 1) * HALF)
+            quantize(cast(interleave, result[h][:], 88), out_codes[:, cols], out_scales[:, cols], E4M3)
+            nc.sync.dma_start(out=words[:, cols], in_=out_codes[:, cols].bitcast(I32))
+
+        run(interleave_dealt, x_raw, x_q, E4M3, 2, 3, nothing)
+        late_quantize(2, 0, cast(interleave, late_raw[2, 0], 88))
+        second_product(1, 1, (2, 3))
+        run(interleave_dealt, x_raw, x_q, E4M3, 3, 4, nothing)
+        late_quantize(3, 0, cast(interleave, late_raw[3, 0], 88))
+        late_quantize(2, 1, cast(interleave, late_raw[2, 1], 88))
+        for r in range(3):
+            drain(0, r)
+        late_quantize(3, 1, cast(interleave, late_raw[3, 1], 64))
+        drain(0, 3)
+        store_result(0, 0, 4)
+        quantize_result(0)
+        drain(1, 0)
+        drain(1, 1)
+        store_result(1, 0, 2)
+        drain(1, 2)
+        drain(1, 3)
+        store_result(1, 2, 4)
+        quantize_result(1)
+        for q in range(4):
+            queue = nc.sync if q < 2 else nc.scalar
+            queue.dma_start(out=scale_rows[4 * q : 4 * q + 4, :], in_=out_scales[32 * q : 32 * q + 4, :].bitcast(I32))

@@ -114,10 +114,10 @@ def tile_mix_jvp_tm_pl_none_kernel(tc, w, xd, wd, x, out_0, out_1, out_2):
                     stop=stop,
                 )
 
-        def run(kind, raws, quants, fmt, g0, g1, after):
+        def run(kind, raws, quants, fmt, g0, g1, after, on_scalar=240):
             pending = None
             for g in range(g0, g1 + 1):
-                grouped = cast(kind, raws[g], 256) if g < g1 else None
+                grouped = cast(kind, raws[g], on_scalar) if g < g1 else None
                 if pending is not None:
                     quantize(pending, quants[g - 1][0][:], quants[g - 1][1][:], fmt)
                     after(g - 1)
@@ -137,12 +137,11 @@ def tile_mix_jvp_tm_pl_none_kernel(tc, w, xd, wd, x, out_0, out_1, out_2):
         run(interleave, w_raw, w_q, E4M3, 0, 2, first_product)
         run(interleave, w_raw, w_q, E4M3, 2, 4, first_product)
         run(interleave_dealt, x_raw, x_q, E4M3, 0, 2, nothing)
-        run(interleave, wd_raw, wd_q, E5M2, 0, 1, nothing)
+        run(interleave, wd_raw, wd_q, E5M2, 0, 1, nothing, 176)
         second_product(0, 0)
         second_product(0, 1)
-        run(interleave, wd_raw, wd_q, E5M2, 1, 2, nothing)
+        run(interleave, wd_raw, wd_q, E5M2, 1, 2, nothing, 176)
         second_product(1, 0)
-        second_product(1, 1, (0, 1))
 
         def late_quantize(g, h, grouped):
             cols = slice(2 * h * HALF, (2 * h + 1) * HALF)
@@ -150,8 +149,8 @@ def tile_mix_jvp_tm_pl_none_kernel(tc, w, xd, wd, x, out_0, out_1, out_2):
             window = slice(h * HALF, h * HALF + M)
             multiply(h, x_q[g], E4M3, late_q[g][0][:, window], late_q[g][1][:, window], E5M2, False, g == 3)
 
-        def drain(h, r):
-            nc.scalar.copy(out=result[h][:, r, :], in_=banks[h][r][:, h * HALF : (h + 1) * HALF])
+        def drain(h, r, copy=nc.scalar.copy):
+            copy(out=result[h][:, r, :], in_=banks[h][r][:, h * HALF : (h + 1) * HALF])
 
         def store_result(h, r0, r1):
             nc.sync.dma_start(
@@ -167,22 +166,26 @@ def tile_mix_jvp_tm_pl_none_kernel(tc, w, xd, wd, x, out_0, out_1, out_2):
             quantize(cast(interleave, result[h][:], 88), out_codes[:, cols], out_scales[:, cols], E4M3)
             nc.sync.dma_start(out=words[:, cols], in_=out_codes[:, cols].bitcast(I32))
 
-        run(interleave_dealt, x_raw, x_q, E4M3, 2, 3, nothing)
-        late_quantize(2, 0, cast(interleave, late_raw[2, 0], 88))
-        second_product(1, 1, (2, 3))
-        run(interleave_dealt, x_raw, x_q, E4M3, 3, 4, nothing)
-        late_quantize(3, 0, cast(interleave, late_raw[3, 0], 88))
-        late_quantize(2, 1, cast(interleave, late_raw[2, 1], 88))
-        for r in range(3):
+        run(interleave_dealt, x_raw, x_q, E4M3, 2, 3, nothing, 176)
+        late_quantize(2, 0, cast(interleave, late_raw[2, 0], 144))
+        second_product(1, 1)
+        x3_grouped = cast(interleave_dealt, x_raw[3], 176)
+        quantize(x3_grouped[:, : PACK * HALF], x_q[3][0][:, :HALF], x_q[3][1][:, :HALF], E4M3)
+        grouped = cast(interleave, late_raw[3, 0], 144)
+        quantize(grouped, late_q[3][0][:, :HALF], late_q[3][1][:, :HALF], E5M2)
+        quantize(x3_grouped[:, PACK * HALF :], x_q[3][0][:, HALF:], x_q[3][1][:, HALF:], E4M3)
+        multiply(0, x_q[3], E4M3, late_q[3][0][:, :M], late_q[3][1][:, :M], E5M2, False, True)
+        late_quantize(2, 1, cast(interleave, late_raw[2, 1], 112))
+        drain(0, 0)
+        late_quantize(3, 1, cast(interleave, late_raw[3, 1], 112))
+        for r in range(1, 4):
             drain(0, r)
-        late_quantize(3, 1, cast(interleave, late_raw[3, 1], 64))
-        drain(0, 3)
         store_result(0, 0, 4)
         quantize_result(0)
         drain(1, 0)
         drain(1, 1)
         store_result(1, 0, 2)
-        drain(1, 2)
+        drain(1, 2, nc.vector.tensor_copy)
         drain(1, 3)
         store_result(1, 2, 4)
         quantize_result(1)

@@ -87,8 +87,8 @@ def tile_mix_jvp_tm_pl_none_kernel(tc, w, xd, wd, x, out_0, out_1, out_2):
 
         def interleave_dealt(copy, grouped, raw, c0, c1):
             copy(
-                out=grouped[:].rearrange("p (r m j) -> p m r j", r=PACK, j=PACK)[:, c0 // PACK : c1 // PACK, :, :],
-                in_=raw[:, :, c0:c1].rearrange("p j (m r) -> p m r j", r=PACK),
+                out=grouped[:].rearrange("p (r m j) -> p m j r", r=PACK, j=PACK)[:, c0 // PACK : c1 // PACK, :, :],
+                in_=raw[:, :, c0:c1].rearrange("p j (m r) -> p m j r", r=PACK),
             )
 
         def cast(kind, raw, on_scalar):
@@ -169,17 +169,19 @@ def tile_mix_jvp_tm_pl_none_kernel(tc, w, xd, wd, x, out_0, out_1, out_2):
         run(interleave_dealt, x_raw, x_q, E4M3, 2, 3, nothing, 176)
         late_quantize(2, 0, cast(interleave, late_raw[2, 0], 144))
         second_product(1, 1)
-        x3_grouped = cast(interleave_dealt, x_raw[3], 176)
+        x3_grouped = cast(interleave_dealt, x_raw[3], 184)
+        grouped = cast(interleave, late_raw[3, 0], 88)
         quantize(x3_grouped[:, : PACK * HALF], x_q[3][0][:, :HALF], x_q[3][1][:, :HALF], E4M3)
-        grouped = cast(interleave, late_raw[3, 0], 144)
         quantize(grouped, late_q[3][0][:, :HALF], late_q[3][1][:, :HALF], E5M2)
         quantize(x3_grouped[:, PACK * HALF :], x_q[3][0][:, HALF:], x_q[3][1][:, HALF:], E4M3)
         multiply(0, x_q[3], E4M3, late_q[3][0][:, :M], late_q[3][1][:, :M], E5M2, False, True)
-        late_quantize(2, 1, cast(interleave, late_raw[2, 1], 112))
+        late_quantize(2, 1, cast(interleave, late_raw[2, 1], 144))
         drain(0, 0)
-        late_quantize(3, 1, cast(interleave, late_raw[3, 1], 112))
-        for r in range(1, 4):
-            drain(0, r)
+        grouped = cast(interleave, late_raw[3, 1], 104)
+        drain(0, 3, nc.vector.tensor_copy)
+        late_quantize(3, 1, grouped)
+        drain(0, 1)
+        drain(0, 2)
         store_result(0, 0, 4)
         quantize_result(0)
         drain(1, 0)

@@ -50,12 +50,10 @@ def tile_mix_jvp_tm_pl_none_kernel(tc, w, xd, wd, x, out_0, out_1, out_2):
         x_raw = load_passes("x_raw01", x, 0, 2)
         wd_raw = load_passes("wd_raw0", wd, 0, 1)
         wd_raw = wd_raw + load_passes("wd_raw1", wd, 1, 2)
-        late_raw = {}
-        for g in (2, 3):
-            x_raw = x_raw + load_passes("x_raw%d" % g, x, g, g + 1)
-            late_raw[g, 0] = load_half("wd_raw%d_0" % g, wd, g, 0)
-        for g in (2, 3):
-            late_raw[g, 1] = load_half("wd_raw%d_1" % g, wd, g, 1)
+        x_raw = x_raw + load_passes("x_raw2", x, 2, 3)
+        wd_raw = wd_raw + load_passes("wd_raw2", wd, 2, 3)
+        x_raw = x_raw + load_passes("x_raw3", x, 3, 4)
+        late_raw = {(3, h): load_half("wd_raw3_%d" % h, wd, 3, h) for h in range(2)}
 
         def mx_tiles(name, width):
             codes = keep.tile([P, width], U32, name=name + "_codes", align_bytes=64)
@@ -65,9 +63,9 @@ def tile_mix_jvp_tm_pl_none_kernel(tc, w, xd, wd, x, out_0, out_1, out_2):
         xd_q = [mx_tiles("xd%d" % g, T) for g in range(PASSES)]
         w_q = [mx_tiles("w%d" % g, M) for g in range(PASSES)]
         x_q = [mx_tiles("x%d" % g, T) for g in range(PASSES)]
-        wd_q = [mx_tiles("wd%d" % g, M) for g in range(2)]
-        late_q = {g: mx_tiles("wd%d" % g, 3 * HALF) for g in (2, 3)}
-        for g in (2, 3):
+        wd_q = [mx_tiles("wd%d" % g, M) for g in range(3)]
+        late_q = {g: mx_tiles("wd%d" % g, 3 * HALF) for g in (3,)}
+        for g in (3,):
             nc.vector.memset(late_q[g][0][:, HALF : 2 * HALF], 0)
             nc.vector.memset(late_q[g][1][:, HALF : 2 * HALF].bitcast(U32), 0)
 
@@ -161,36 +159,44 @@ def tile_mix_jvp_tm_pl_none_kernel(tc, w, xd, wd, x, out_0, out_1, out_2):
         words = out_1[0].rearrange("p n i -> p (n i)").bitcast(I32)
         scale_rows = out_2[0].bitcast(I32)
 
-        def quantize_result(h):
+        def quantize_result(h, on_scalar):
             cols = slice(h * HALF, (h + 1) * HALF)
-            quantize(cast(interleave, result[h][:], 88), out_codes[:, cols], out_scales[:, cols], E4M3)
+            quantize(cast(interleave, result[h][:], on_scalar), out_codes[:, cols], out_scales[:, cols], E4M3)
+
+        def store_words(h):
+            cols = slice(h * HALF, (h + 1) * HALF)
             nc.sync.dma_start(out=words[:, cols], in_=out_codes[:, cols].bitcast(I32))
 
-        run(interleave_dealt, x_raw, x_q, E4M3, 2, 3, nothing, 176)
-        late_quantize(2, 0, cast(interleave, late_raw[2, 0], 144))
         second_product(1, 1)
+        run(interleave_dealt, x_raw, x_q, E4M3, 2, 3, nothing, 176)
+        run(interleave, wd_raw, wd_q, E5M2, 2, 3, nothing, 176)
+        second_product(2, 0)
+        second_product(2, 1)
         x3_grouped = cast(interleave_dealt, x_raw[3], 184)
         grouped = cast(interleave, late_raw[3, 0], 88)
         quantize(x3_grouped[:, : PACK * HALF], x_q[3][0][:, :HALF], x_q[3][1][:, :HALF], E4M3)
         quantize(grouped, late_q[3][0][:, :HALF], late_q[3][1][:, :HALF], E5M2)
         quantize(x3_grouped[:, PACK * HALF :], x_q[3][0][:, HALF:], x_q[3][1][:, HALF:], E4M3)
         multiply(0, x_q[3], E4M3, late_q[3][0][:, :M], late_q[3][1][:, :M], E5M2, False, True)
-        late_quantize(2, 1, cast(interleave, late_raw[2, 1], 144))
+        late_quantize(3, 1, cast(interleave, late_raw[3, 1], 144))
         drain(0, 0)
-        grouped = cast(interleave, late_raw[3, 1], 104)
-        drain(0, 3, nc.vector.tensor_copy)
-        late_quantize(3, 1, grouped)
         drain(0, 1)
-        drain(0, 2)
-        store_result(0, 0, 4)
-        quantize_result(0)
+        store_result(0, 0, 2)
+        drain(0, 2, nc.vector.tensor_copy)
+        drain(0, 3)
+        store_result(0, 2, 4)
+        left_grouped = new_grouped()
+        interleave(nc.vector.tensor_copy, left_grouped, result[0][:], 0, HALF)
         drain(1, 0)
         drain(1, 1)
         store_result(1, 0, 2)
         drain(1, 2, nc.vector.tensor_copy)
         drain(1, 3)
+        quantize(left_grouped[:, : PACK * HALF], out_codes[:, :HALF], out_scales[:, :HALF], E4M3)
         store_result(1, 2, 4)
-        quantize_result(1)
+        store_words(0)
+        quantize_result(1, 104)
+        store_words(1)
         for q in range(4):
             queue = nc.sync if q < 2 else nc.scalar
             queue.dma_start(out=scale_rows[4 * q : 4 * q + 4, :], in_=out_scales[32 * q : 32 * q + 4, :].bitcast(I32))

@@ -172,16 +172,17 @@ def tile_mix_jvp_tm_pl_none_kernel(tc, w, xd, wd, x, out_0, out_1, out_2):
         run(interleave, wd_raw, wd_q, E5M2, 2, 3, nothing, 176)
         second_product(2, 0)
         second_product(2, 1)
-        x3_grouped = cast(interleave_dealt, x_raw[3], 184)
-        grouped = cast(interleave, late_raw[3, 0], 88)
+        x3_grouped = cast(interleave_dealt, x_raw[3], 176)
+        grouped = cast(interleave, late_raw[3, 0], 80)
         quantize(x3_grouped[:, : PACK * HALF], x_q[3][0][:, :HALF], x_q[3][1][:, :HALF], E4M3)
         quantize(grouped, late_q[3][0][:, :HALF], late_q[3][1][:, :HALF], E5M2)
         quantize(x3_grouped[:, PACK * HALF :], x_q[3][0][:, HALF:], x_q[3][1][:, HALF:], E4M3)
         multiply(0, x_q[3], E4M3, late_q[3][0][:, :M], late_q[3][1][:, :M], E5M2, False, True)
-        late_quantize(3, 1, cast(interleave, late_raw[3, 1], 144))
+        late_quantize(3, 1, cast(interleave, late_raw[3, 1], 120))
         drain(0, 0)
+        store_result(0, 0, 1)
         drain(0, 1)
-        store_result(0, 0, 2)
+        store_result(0, 1, 2)
         drain(0, 2, nc.vector.tensor_copy)
         drain(0, 3)
         store_result(0, 2, 4)

@@ -24,7 +24,7 @@ def tile_mix_jvp_tm_pl_none_kernel(tc, w, xd, wd, x, out_0, out_1, out_2):
     nc = tc.nc
     with ExitStack() as ctx:
         keep = ctx.enter_context(tc.tile_pool(name="keep", bufs=1))
-        stage = ctx.enter_context(tc.tile_pool(name="stage", bufs=4))
+        stage = ctx.enter_context(tc.tile_pool(name="stage", bufs=6))
         psum = ctx.enter_context(tc.psum_pool(name="psum", bufs=1))
         ctx.enter_context(tc.manual_schedule())
 
@@ -87,6 +87,13 @@ def tile_mix_jvp_tm_pl_none_kernel(tc, w, xd, wd, x, out_0, out_1, out_2):
             copy(
                 out=grouped[:].rearrange("p (r m j) -> p m j r", r=PACK, j=PACK)[:, c0 // PACK : c1 // PACK, :, :],
                 in_=raw[:, :, c0:c1].rearrange("p j (m r) -> p m j r", r=PACK),
+            )
+
+        def deal_pair(copy, grouped, raw, pair, m0, m1):
+            rs = slice(2 * pair, 2 * pair + 2)
+            copy(
+                out=grouped[:].rearrange("p (r m j) -> p m j r", r=PACK, j=PACK)[:, m0:m1, :, rs],
+                in_=raw.rearrange("p j (m r) -> p m j r", r=PACK)[:, m0:m1, :, rs],
             )
 
         def cast(kind, raw, on_scalar):
@@ -172,31 +179,43 @@ def tile_mix_jvp_tm_pl_none_kernel(tc, w, xd, wd, x, out_0, out_1, out_2):
         run(interleave, wd_raw, wd_q, E5M2, 2, 3, nothing, 176)
         second_product(2, 0)
         second_product(2, 1)
-        x3_grouped = cast(interleave_dealt, x_raw[3], 176)
-        grouped = cast(interleave, late_raw[3, 0], 80)
+        x3_grouped = new_grouped()
+        deal_pair(nc.vector.tensor_copy, x3_grouped, x_raw[3], 0, 0, P)
+        deal_pair(nc.scalar.copy, x3_grouped, x_raw[3], 1, 0, 80)
+        deal_pair(nc.vector.tensor_copy, x3_grouped, x_raw[3], 1, 80, P)
         quantize(x3_grouped[:, : PACK * HALF], x_q[3][0][:, :HALF], x_q[3][1][:, :HALF], E4M3)
-        quantize(grouped, late_q[3][0][:, :HALF], late_q[3][1][:, :HALF], E5M2)
+        grouped = cast(interleave, late_raw[3, 0], 112)
         quantize(x3_grouped[:, PACK * HALF :], x_q[3][0][:, HALF:], x_q[3][1][:, HALF:], E4M3)
+        quantize(grouped, late_q[3][0][:, :HALF], late_q[3][1][:, :HALF], E5M2)
         multiply(0, x_q[3], E4M3, late_q[3][0][:, :M], late_q[3][1][:, :M], E5M2, False, True)
-        late_quantize(3, 1, cast(interleave, late_raw[3, 1], 120))
+        late_quantize(3, 1, cast(interleave, late_raw[3, 1], 96))
         drain(0, 0)
         store_result(0, 0, 1)
         drain(0, 1)
         store_result(0, 1, 2)
         drain(0, 2, nc.vector.tensor_copy)
-        drain(0, 3)
-        store_result(0, 2, 4)
+        quarter = HALF // 2
         left_grouped = new_grouped()
-        interleave(nc.vector.tensor_copy, left_grouped, result[0][:], 0, HALF)
+        for c in range(2):
+            nc.scalar.copy(out=result[0][:, 3, c * quarter : (c + 1) * quarter], in_=banks[0][3][:, c * quarter : (c + 1) * quarter])
+            interleave(nc.vector.tensor_copy, left_grouped, result[0][:], c * quarter, (c + 1) * quarter)
+        store_result(0, 2, 4)
         drain(1, 0)
         drain(1, 1)
         store_result(1, 0, 2)
-        drain(1, 2, nc.vector.tensor_copy)
-        drain(1, 3)
+        drain(1, 2)
         quantize(left_grouped[:, : PACK * HALF], out_codes[:, :HALF], out_scales[:, :HALF], E4M3)
-        store_result(1, 2, 4)
+        for c in range(2):
+            nc.scalar.copy(out=result[1][:, 3, c * quarter : (c + 1) * quarter], in_=banks[1][3][:, HALF + c * quarter : HALF + (c + 1) * quarter])
         store_words(0)
-        quantize_result(1, 104)
+        store_result(1, 2, 4)
+        grouped = new_grouped()
+        interleave(nc.vector.tensor_copy, grouped, result[1][:], 0, quarter)
+        interleave(nc.scalar.copy, grouped, result[1][:], quarter, quarter + 64)
+        interleave(nc.vector.tensor_copy, grouped, result[1][:], quarter + 64, HALF)
+        for c in range(2):
+            cols = slice(HALF + c * quarter, HALF + (c + 1) * quarter)
+            quantize(grouped[:, c * PACK * quarter : (c + 1) * PACK * quarter], out_codes[:, cols], out_scales[:, cols], E4M3)
         store_words(1)
         for q in range(4):
             queue = nc.sync if q < 2 else nc.scalar

@@ -181,14 +181,14 @@ def tile_mix_jvp_tm_pl_none_kernel(tc, w, xd, wd, x, out_0, out_1, out_2):
         second_product(2, 1)
         x3_grouped = new_grouped()
         deal_pair(nc.vector.tensor_copy, x3_grouped, x_raw[3], 0, 0, P)
-        deal_pair(nc.scalar.copy, x3_grouped, x_raw[3], 1, 0, 80)
-        deal_pair(nc.vector.tensor_copy, x3_grouped, x_raw[3], 1, 80, P)
+        deal_pair(nc.scalar.copy, x3_grouped, x_raw[3], 1, 0, 56)
+        deal_pair(nc.vector.tensor_copy, x3_grouped, x_raw[3], 1, 56, P)
         quantize(x3_grouped[:, : PACK * HALF], x_q[3][0][:, :HALF], x_q[3][1][:, :HALF], E4M3)
-        grouped = cast(interleave, late_raw[3, 0], 112)
+        grouped = cast(interleave, late_raw[3, 0], 64)
         quantize(x3_grouped[:, PACK * HALF :], x_q[3][0][:, HALF:], x_q[3][1][:, HALF:], E4M3)
         quantize(grouped, late_q[3][0][:, :HALF], late_q[3][1][:, :HALF], E5M2)
         multiply(0, x_q[3], E4M3, late_q[3][0][:, :M], late_q[3][1][:, :M], E5M2, False, True)
-        late_quantize(3, 1, cast(interleave, late_raw[3, 1], 96))
+        late_quantize(3, 1, cast(interleave, late_raw[3, 1], 64))
         drain(0, 0)
         store_result(0, 0, 1)
         drain(0, 1)
@@ -211,8 +211,8 @@ def tile_mix_jvp_tm_pl_none_kernel(tc, w, xd, wd, x, out_0, out_1, out_2):
         store_result(1, 2, 4)
         grouped = new_grouped()
         interleave(nc.vector.tensor_copy, grouped, result[1][:], 0, quarter)
-        interleave(nc.scalar.copy, grouped, result[1][:], quarter, quarter + 64)
-        interleave(nc.vector.tensor_copy, grouped, result[1][:], quarter + 64, HALF)
+        interleave(nc.scalar.copy, grouped, result[1][:], quarter, quarter + 32)
+        interleave(nc.vector.tensor_copy, grouped, result[1][:], quarter + 32, HALF)
         for c in range(2):
             cols = slice(HALF + c * quarter, HALF + (c + 1) * quarter)
             quantize(grouped[:, c * PACK * quarter : (c + 1) * PACK * quarter], out_codes[:, cols], out_scales[:, cols], E4M3)

@@ -207,8 +207,8 @@ def tile_mix_jvp_tm_pl_none_kernel(tc, w, xd, wd, x, out_0, out_1, out_2):
         quantize(left_grouped[:, : PACK * HALF], out_codes[:, :HALF], out_scales[:, :HALF], E4M3)
         for c in range(2):
             nc.scalar.copy(out=result[1][:, 3, c * quarter : (c + 1) * quarter], in_=banks[1][3][:, HALF + c * quarter : HALF + (c + 1) * quarter])
-        store_words(0)
         store_result(1, 2, 4)
+        store_words(0)
         grouped = new_grouped()
         interleave(nc.vector.tensor_copy, grouped, result[1][:], 0, quarter)
         interleave(nc.scalar.copy, grouped, result[1][:], quarter, quarter + 32)

@@ -29,7 +29,7 @@ def tile_mix_jvp_tm_pl_none_kernel(tc, w, xd, wd, x, out_0, out_1, out_2):
         ctx.enter_context(tc.manual_schedule())
 
         def load_passes(name, src, g0, g1):
-            raw = keep.tile([P, g1 - g0, PACK, M], F32, name=name)
+            raw = keep.tile([P, g1 - g0, PACK, M], F32, name=name, align_bytes=256)
             nc.sync.dma_start(
                 out=raw[:].rearrange("p g j n -> p g (j n)"),
                 in_=src[g0 * K_PASS : g1 * K_PASS, :].rearrange("(g p j) n -> p g (j n)", p=P, j=PACK),
@@ -37,7 +37,7 @@ def tile_mix_jvp_tm_pl_none_kernel(tc, w, xd, wd, x, out_0, out_1, out_2):
             return [raw[:, g, :, :] for g in range(g1 - g0)]
 
         def load_half(name, src, g, h):
-            raw = keep.tile([P, PACK, HALF], F32, name=name)
+            raw = keep.tile([P, PACK, HALF], F32, name=name, align_bytes=256)
             nc.sync.dma_start(
                 out=raw[:],
                 in_=src[g * K_PASS : (g + 1) * K_PASS, h * HALF : (h + 1) * HALF].rearrange("(p j) n -> p j n", j=PACK),
@@ -56,8 +56,8 @@ def tile_mix_jvp_tm_pl_none_kernel(tc, w, xd, wd, x, out_0, out_1, out_2):
         late_raw = {(3, h): load_half("wd_raw3_%d" % h, wd, 3, h) for h in range(2)}
 
         def mx_tiles(name, width):
-            codes = keep.tile([P, width], U32, name=name + "_codes", align_bytes=64)
-            scales = keep.tile([P, width], U8, name=name + "_scales", align_bytes=64)
+            codes = keep.tile([P, width], U32, name=name + "_codes", align_bytes=256)
+            scales = keep.tile([P, width], U8, name=name + "_scales", align_bytes=256)
             return codes, scales
 
         xd_q = [mx_tiles("xd%d" % g, T) for g in range(PASSES)]
@@ -70,11 +70,11 @@ def tile_mix_jvp_tm_pl_none_kernel(tc, w, xd, wd, x, out_0, out_1, out_2):
             nc.vector.memset(late_q[g][1][:, HALF : 2 * HALF].bitcast(U32), 0)
 
         banks = [[psum.tile([P, M], F32, name="acc%d_%d" % (h, r)) for r in range(PACK)] for h in range(2)]
-        result = [keep.tile([P, PACK, HALF], F32, name="result%d" % h) for h in range(2)]
+        result = [keep.tile([P, PACK, HALF], F32, name="result%d" % h, align_bytes=256) for h in range(2)]
         out_codes, out_scales = mx_tiles("out", M)
 
         def new_grouped():
-            grouped = stage.tile([P, PACK * M], BF16, name="grouped", align_bytes=64)
+            grouped = stage.tile([P, PACK * M], BF16, name="grouped", align_bytes=256)
             return grouped
 
         def interleave(copy, grouped, raw, c0, c1):

@@ -51,9 +51,10 @@ def tile_mix_jvp_tm_pl_none_kernel(tc, w, xd, wd, x, out_0, out_1, out_2):
         wd_raw = load_passes("wd_raw0", wd, 0, 1)
         wd_raw = wd_raw + load_passes("wd_raw1", wd, 1, 2)
         x_raw = x_raw + load_passes("x_raw2", x, 2, 3)
-        wd_raw = wd_raw + load_passes("wd_raw2", wd, 2, 3)
+        late_raw = {(2, 0): load_half("wd_raw2_0", wd, 2, 0)}
         x_raw = x_raw + load_passes("x_raw3", x, 3, 4)
-        late_raw = {(3, h): load_half("wd_raw3_%d" % h, wd, 3, h) for h in range(2)}
+        for g, h in ((3, 0), (2, 1), (3, 1)):
+            late_raw.setdefault((g, h), load_half("wd_raw%d_%d" % (g, h), wd, g, h))
 
         def mx_tiles(name, width):
             codes = keep.tile([P, width], U32, name=name + "_codes", align_bytes=256)
@@ -63,9 +64,9 @@ def tile_mix_jvp_tm_pl_none_kernel(tc, w, xd, wd, x, out_0, out_1, out_2):
         xd_q = [mx_tiles("xd%d" % g, T) for g in range(PASSES)]
         w_q = [mx_tiles("w%d" % g, M) for g in range(PASSES)]
         x_q = [mx_tiles("x%d" % g, T) for g in range(PASSES)]
-        wd_q = [mx_tiles("wd%d" % g, M) for g in range(3)]
-        late_q = {g: mx_tiles("wd%d" % g, 3 * HALF) for g in (3,)}
-        for g in (3,):
+        wd_q = [mx_tiles("wd%d" % g, M) for g in range(2)]
+        late_q = {g: mx_tiles("wd%d" % g, 3 * HALF) for g in (2, 3)}
+        for g in (2, 3):
             nc.vector.memset(late_q[g][0][:, HALF : 2 * HALF], 0)
             nc.vector.memset(late_q[g][1][:, HALF : 2 * HALF].bitcast(U32), 0)
 
@@ -166,53 +167,48 @@ def tile_mix_jvp_tm_pl_none_kernel(tc, w, xd, wd, x, out_0, out_1, out_2):
         words = out_1[0].rearrange("p n i -> p (n i)").bitcast(I32)
         scale_rows = out_2[0].bitcast(I32)
 
-        def quantize_result(h, on_scalar):
-            cols = slice(h * HALF, (h + 1) * HALF)
-            quantize(cast(interleave, result[h][:], on_scalar), out_codes[:, cols], out_scales[:, cols], E4M3)
-
         def store_words(h):
             cols = slice(h * HALF, (h + 1) * HALF)
             nc.sync.dma_start(out=words[:, cols], in_=out_codes[:, cols].bitcast(I32))
 
-        second_product(1, 1)
         run(interleave_dealt, x_raw, x_q, E4M3, 2, 3, nothing, 176)
-        run(interleave, wd_raw, wd_q, E5M2, 2, 3, nothing, 176)
-        second_product(2, 0)
-        second_product(2, 1)
+        late_quantize(2, 0, cast(interleave, late_raw[2, 0], 88))
+        second_product(1, 1)
         x3_grouped = new_grouped()
         deal_pair(nc.vector.tensor_copy, x3_grouped, x_raw[3], 0, 0, P)
-        deal_pair(nc.scalar.copy, x3_grouped, x_raw[3], 1, 0, 56)
-        deal_pair(nc.vector.tensor_copy, x3_grouped, x_raw[3], 1, 56, P)
+        deal_pair(nc.scalar.copy, x3_grouped, x_raw[3], 1, 0, 80)
+        deal_pair(nc.vector.tensor_copy, x3_grouped, x_raw[3], 1, 80, P)
         quantize(x3_grouped[:, : PACK * HALF], x_q[3][0][:, :HALF], x_q[3][1][:, :HALF], E4M3)
-        grouped = cast(interleave, late_raw[3, 0], 64)
+        grouped = cast(interleave, late_raw[3, 0], 104)
         quantize(x3_grouped[:, PACK * HALF :], x_q[3][0][:, HALF:], x_q[3][1][:, HALF:], E4M3)
         quantize(grouped, late_q[3][0][:, :HALF], late_q[3][1][:, :HALF], E5M2)
         multiply(0, x_q[3], E4M3, late_q[3][0][:, :M], late_q[3][1][:, :M], E5M2, False, True)
-        late_quantize(3, 1, cast(interleave, late_raw[3, 1], 64))
+        late_quantize(2, 1, cast(interleave, late_raw[2, 1], 88))
         drain(0, 0)
         store_result(0, 0, 1)
-        drain(0, 1)
+        grouped = cast(interleave, late_raw[3, 1], 88)
+        drain(0, 1, nc.vector.tensor_copy)
         store_result(0, 1, 2)
-        drain(0, 2, nc.vector.tensor_copy)
-        quarter = HALF // 2
-        left_grouped = new_grouped()
-        for c in range(2):
-            nc.scalar.copy(out=result[0][:, 3, c * quarter : (c + 1) * quarter], in_=banks[0][3][:, c * quarter : (c + 1) * quarter])
-            interleave(nc.vector.tensor_copy, left_grouped, result[0][:], c * quarter, (c + 1) * quarter)
-        store_result(0, 2, 4)
+        late_quantize(3, 1, grouped)
+        drain(0, 2)
+        store_result(0, 2, 3)
+        drain(0, 3)
+        store_result(0, 3, 4)
+        left_grouped = cast(interleave, result[0][:], 88)
         drain(1, 0)
+        quantize(left_grouped, out_codes[:, :HALF], out_scales[:, :HALF], E4M3)
+        store_words(0)
         drain(1, 1)
         store_result(1, 0, 2)
-        drain(1, 2)
-        quantize(left_grouped[:, : PACK * HALF], out_codes[:, :HALF], out_scales[:, :HALF], E4M3)
+        drain(1, 2, nc.vector.tensor_copy)
+        quarter = HALF // 2
         for c in range(2):
             nc.scalar.copy(out=result[1][:, 3, c * quarter : (c + 1) * quarter], in_=banks[1][3][:, HALF + c * quarter : HALF + (c + 1) * quarter])
         store_result(1, 2, 4)
-        store_words(0)
         grouped = new_grouped()
         interleave(nc.vector.tensor_copy, grouped, result[1][:], 0, quarter)
-        interleave(nc.scalar.copy, grouped, result[1][:], quarter, quarter + 32)
-        interleave(nc.vector.tensor_copy, grouped, result[1][:], quarter + 32, HALF)
+        interleave(nc.scalar.copy, grouped, result[1][:], quarter, quarter + 64)
+        interleave(nc.vector.tensor_copy, grouped, result[1][:], quarter + 64, HALF)
         for c in range(2):
             cols = slice(HALF + c * quarter, HALF + (c + 1) * quarter)
             quantize(grouped[:, c * PACK * quarter : (c + 1) * PACK * quarter], out_codes[:, cols], out_scales[:, cols], E4M3)

@@ -65,10 +65,7 @@ def tile_mix_jvp_tm_pl_none_kernel(tc, w, xd, wd, x, out_0, out_1, out_2):
         w_q = [mx_tiles("w%d" % g, M) for g in range(PASSES)]
         x_q = [mx_tiles("x%d" % g, T) for g in range(PASSES)]
         wd_q = [mx_tiles("wd%d" % g, M) for g in range(2)]
-        late_q = {g: mx_tiles("wd%d" % g, 3 * HALF) for g in (2, 3)}
-        for g in (2, 3):
-            nc.vector.memset(late_q[g][0][:, HALF : 2 * HALF], 0)
-            nc.vector.memset(late_q[g][1][:, HALF : 2 * HALF].bitcast(U32), 0)
+        late_q = {g: mx_tiles("wd%d" % g, M) for g in (2, 3)}
 
         banks = [[psum.tile([P, M], F32, name="acc%d_%d" % (h, r)) for r in range(PACK)] for h in range(2)]
         result = [keep.tile([P, PACK, HALF], F32, name="result%d" % h, align_bytes=256) for h in range(2)]
@@ -120,6 +117,20 @@ def tile_mix_jvp_tm_pl_none_kernel(tc, w, xd, wd, x, out_0, out_1, out_2):
                     stop=stop,
                 )
 
+        def multiply_half(h, stat, mov, stop):
+            half = slice(h * HALF, (h + 1) * HALF)
+            for r in range(PACK):
+                cols = slice(r * P, (r + 1) * P)
+                nc.tensor.matmul_mx(
+                    out=banks[h][r][:, half],
+                    lhsT=stat[0][:, cols].bitcast(E4M3),
+                    lhsT_scale=stat[1][:, cols],
+                    rhs=mov[0][:, half].bitcast(E5M2),
+                    rhs_scale=mov[1][:, half],
+                    start=False,
+                    stop=stop,
+                )
+
         def run(kind, raws, quants, fmt, g0, g1, after, on_scalar=240):
             pending = None
             for g in range(g0, g1 + 1):
@@ -150,10 +161,9 @@ def tile_mix_jvp_tm_pl_none_kernel(tc, w, xd, wd, x, out_0, out_1, out_2):
         second_product(1, 0)
 
         def late_quantize(g, h, grouped):
-            cols = slice(2 * h * HALF, (2 * h + 1) * HALF)
+            cols = slice(h * HALF, (h + 1) * HALF)
             quantize(grouped, late_q[g][0][:, cols], late_q[g][1][:, cols], E5M2)
-            window = slice(h * HALF, h * HALF + M)
-            multiply(h, x_q[g], E4M3, late_q[g][0][:, window], late_q[g][1][:, window], E5M2, False, g == 3)
+            multiply_half(h, x_q[g], late_q[g], g == 3)
 
         def drain(h, r, copy=nc.scalar.copy):
             copy(out=result[h][:, r, :], in_=banks[h][r][:, h * HALF : (h + 1) * HALF])
@@ -182,7 +192,7 @@ def tile_mix_jvp_tm_pl_none_kernel(tc, w, xd, wd, x, out_0, out_1, out_2):
         grouped = cast(interleave, late_raw[3, 0], 104)
         quantize(x3_grouped[:, PACK * HALF :], x_q[3][0][:, HALF:], x_q[3][1][:, HALF:], E4M3)
         quantize(grouped, late_q[3][0][:, :HALF], late_q[3][1][:, :HALF], E5M2)
-        multiply(0, x_q[3], E4M3, late_q[3][0][:, :M], late_q[3][1][:, :M], E5M2, False, True)
+        multiply_half(0, x_q[3], late_q[3], True)
         late_quantize(2, 1, cast(interleave, late_raw[2, 1], 88))
         drain(0, 0)
         store_result(0, 0, 1)

@@ -18,6 +18,11 @@ PACK = 4
 K_PASS = P * PACK
 PASSES = K // K_PASS
 HALF = M // 2
+QUARTER = M // 4
+LEFT = (0, HALF)
+RIGHT = (HALF, M)
+MID = (HALF, HALF + QUARTER)
+LAST = (HALF + QUARTER, M)
 
 
 def tile_mix_jvp_tm_pl_none_kernel(tc, w, xd, wd, x, out_0, out_1, out_2):
@@ -27,6 +32,8 @@ def tile_mix_jvp_tm_pl_none_kernel(tc, w, xd, wd, x, out_0, out_1, out_2):
         stage = ctx.enter_context(tc.tile_pool(name="stage", bufs=6))
         psum = ctx.enter_context(tc.psum_pool(name="psum", bufs=1))
         ctx.enter_context(tc.manual_schedule())
+        on_scalar = nc.scalar.copy
+        on_vector = nc.vector.tensor_copy
 
         def load_passes(name, src, g0, g1):
             raw = keep.tile([P, g1 - g0, PACK, M], F32, name=name, align_bytes=256)
@@ -36,43 +43,31 @@ def tile_mix_jvp_tm_pl_none_kernel(tc, w, xd, wd, x, out_0, out_1, out_2):
             )
             return [raw[:, g, :, :] for g in range(g1 - g0)]
 
-        def load_half(name, src, g, h):
-            raw = keep.tile([P, PACK, HALF], F32, name=name, align_bytes=256)
+        def load_columns(name, src, g, span):
+            raw = keep.tile([P, PACK, span[1] - span[0]], F32, name=name, align_bytes=256)
             nc.sync.dma_start(
                 out=raw[:],
-                in_=src[g * K_PASS : (g + 1) * K_PASS, h * HALF : (h + 1) * HALF].rearrange("(p j) n -> p j n", j=PACK),
+                in_=src[g * K_PASS : (g + 1) * K_PASS, span[0] : span[1]].rearrange("(p j) n -> p j n", j=PACK),
             )
             return raw[:]
 
-        xd_raw = load_passes("xd_raw", xd, 0, 4)
-        w_raw = load_passes("w_raw01", w, 0, 2)
-        w_raw = w_raw + load_passes("w_raw23", w, 2, 4)
-        x_raw = load_passes("x_raw01", x, 0, 2)
-        wd_raw = load_passes("wd_raw0", wd, 0, 1)
-        wd_raw = wd_raw + load_passes("wd_raw1", wd, 1, 2)
-        x_raw = x_raw + load_passes("x_raw2", x, 2, 3)
-        late_raw = {(2, 0): load_half("wd_raw2_0", wd, 2, 0)}
-        x_raw = x_raw + load_passes("x_raw3", x, 3, 4)
-        for g, h in ((3, 0), (2, 1), (3, 1)):
-            late_raw.setdefault((g, h), load_half("wd_raw%d_%d" % (g, h), wd, g, h))
-
-        def mx_tiles(name, width):
-            codes = keep.tile([P, width], U32, name=name + "_codes", align_bytes=256)
-            scales = keep.tile([P, width], U8, name=name + "_scales", align_bytes=256)
+        def mx_tiles(name):
+            codes = keep.tile([P, M], U32, name=name + "_codes", align_bytes=256)
+            scales = keep.tile([P, M], U8, name=name + "_scales", align_bytes=256)
             return codes, scales
 
-        xd_q = [mx_tiles("xd%d" % g, T) for g in range(PASSES)]
-        w_q = [mx_tiles("w%d" % g, M) for g in range(PASSES)]
-        x_q = [mx_tiles("x%d" % g, T) for g in range(PASSES)]
-        wd_q = [mx_tiles("wd%d" % g, M) for g in range(2)]
-        late_q = {g: mx_tiles("wd%d" % g, M) for g in (2, 3)}
+        xd_q = [mx_tiles("xd%d" % g) for g in range(PASSES)]
+        w_q = [mx_tiles("w%d" % g) for g in range(PASSES)]
+        x_q = [mx_tiles("x%d" % g) for g in range(PASSES)]
+        wd_q = [mx_tiles("wd%d" % g) for g in range(PASSES)]
+        out_q = mx_tiles("out")
 
-        banks = [[psum.tile([P, M], F32, name="acc%d_%d" % (h, r)) for r in range(PACK)] for h in range(2)]
-        result = [keep.tile([P, PACK, HALF], F32, name="result%d" % h, align_bytes=256) for h in range(2)]
-        out_codes, out_scales = mx_tiles("out", M)
-
-        def new_grouped():
+        def whole_grouped():
             grouped = stage.tile([P, PACK * M], BF16, name="grouped", align_bytes=256)
+            return grouped
+
+        def own_grouped(name, width):
+            grouped = keep.tile([P, PACK * width], BF16, name=name, align_bytes=256)
             return grouped
 
         def interleave(copy, grouped, raw, c0, c1):
@@ -87,142 +82,152 @@ def tile_mix_jvp_tm_pl_none_kernel(tc, w, xd, wd, x, out_0, out_1, out_2):
                 in_=raw[:, :, c0:c1].rearrange("p j (m r) -> p m j r", r=PACK),
             )
 
-        def deal_pair(copy, grouped, raw, pair, m0, m1):
-            rs = slice(2 * pair, 2 * pair + 2)
-            copy(
-                out=grouped[:].rearrange("p (r m j) -> p m j r", r=PACK, j=PACK)[:, m0:m1, :, rs],
-                in_=raw.rearrange("p j (m r) -> p m j r", r=PACK)[:, m0:m1, :, rs],
+        def shared(kind, grouped, raw, scalar_columns):
+            kind(on_scalar, grouped, raw, 0, scalar_columns)
+            kind(on_vector, grouped, raw, scalar_columns, raw.shape[2])
+
+        def quantize(grouped, tiles, span, fmt):
+            nc.vector.quantize_mx(
+                out=tiles[0][:, span[0] : span[1]].bitcast(fmt), scales=tiles[1][:, span[0] : span[1]], in_=grouped
             )
 
-        def cast(kind, raw, on_scalar):
-            grouped = new_grouped()
-            width = raw.shape[2]
-            kind(nc.scalar.copy, grouped, raw, 0, on_scalar)
-            kind(nc.vector.tensor_copy, grouped, raw, on_scalar, width)
-            return grouped[:, : PACK * width]
-
-        def quantize(grouped, codes, scales, fmt):
-            nc.vector.quantize_mx(out=codes.bitcast(fmt), scales=scales, in_=grouped)
-
-        def multiply(h, stat, stat_fmt, mov_codes, mov_scales, mov_fmt, start, stop, rs=range(PACK)):
-            for r in rs:
-                cols = slice(r * P, (r + 1) * P)
-                nc.tensor.matmul_mx(
-                    out=banks[h][r][:],
-                    lhsT=stat[0][:, cols].bitcast(stat_fmt),
-                    lhsT_scale=stat[1][:, cols],
-                    rhs=mov_codes.bitcast(mov_fmt),
-                    rhs_scale=mov_scales,
-                    start=start,
-                    stop=stop,
-                )
-
-        def multiply_half(h, stat, mov, stop):
-            half = slice(h * HALF, (h + 1) * HALF)
-            for r in range(PACK):
-                cols = slice(r * P, (r + 1) * P)
-                nc.tensor.matmul_mx(
-                    out=banks[h][r][:, half],
-                    lhsT=stat[0][:, cols].bitcast(E4M3),
-                    lhsT_scale=stat[1][:, cols],
-                    rhs=mov[0][:, half].bitcast(E5M2),
-                    rhs_scale=mov[1][:, half],
-                    start=False,
-                    stop=stop,
-                )
-
-        def run(kind, raws, quants, fmt, g0, g1, after, on_scalar=240):
+        def run(jobs, scalar_columns):
             pending = None
-            for g in range(g0, g1 + 1):
-                grouped = cast(kind, raws[g], on_scalar) if g < g1 else None
+            for job in jobs + [None]:
+                grouped = None
+                if job is not None:
+                    grouped = whole_grouped()
+                    shared(job[0], grouped, job[1], scalar_columns)
                 if pending is not None:
-                    quantize(pending, quants[g - 1][0][:], quants[g - 1][1][:], fmt)
-                    after(g - 1)
-                pending = grouped
+                    quantize(pending[0][:], pending[1][2], (0, M), pending[1][3])
+                    pending[1][4]()
+                pending = (grouped, job)
 
-        def first_product(g):
-            for h in range(2):
-                multiply(h, xd_q[g], E5M2, w_q[g][0][:], w_q[g][1][:], E4M3, g == 0, False)
-
-        def second_product(g, h, rs=range(PACK)):
-            multiply(h, x_q[g], E4M3, wd_q[g][0][:], wd_q[g][1][:], E5M2, False, False, rs)
-
-        def nothing(g):
-            return None
-
-        run(interleave_dealt, xd_raw, xd_q, E5M2, 0, 4, nothing)
-        run(interleave, w_raw, w_q, E4M3, 0, 2, first_product)
-        run(interleave, w_raw, w_q, E4M3, 2, 4, first_product)
-        run(interleave_dealt, x_raw, x_q, E4M3, 0, 2, nothing)
-        run(interleave, wd_raw, wd_q, E5M2, 0, 1, nothing, 176)
-        second_product(0, 0)
-        second_product(0, 1)
-        run(interleave, wd_raw, wd_q, E5M2, 1, 2, nothing, 176)
-        second_product(1, 0)
-
-        def late_quantize(g, h, grouped):
-            cols = slice(h * HALF, (h + 1) * HALF)
-            quantize(grouped, late_q[g][0][:, cols], late_q[g][1][:, cols], E5M2)
-            multiply_half(h, x_q[g], late_q[g], g == 3)
-
-        def drain(h, r, copy=nc.scalar.copy):
-            copy(out=result[h][:, r, :], in_=banks[h][r][:, h * HALF : (h + 1) * HALF])
-
-        def store_result(h, r0, r1):
-            nc.sync.dma_start(
-                out=out_0[:, h * HALF : (h + 1) * HALF].rearrange("(p r) n -> p r n", r=PACK)[:, r0:r1, :],
-                in_=result[h][:, r0:r1, :],
+        def matmul(out, stat, stat_fmt, r, mov, mov_fmt, span, start, stop):
+            cols = slice(r * P, (r + 1) * P)
+            nc.tensor.matmul_mx(
+                out=out,
+                lhsT=stat[0][:, cols].bitcast(stat_fmt),
+                lhsT_scale=stat[1][:, cols],
+                rhs=mov[0][:, span[0] : span[1]].bitcast(mov_fmt),
+                rhs_scale=mov[1][:, span[0] : span[1]],
+                start=start,
+                stop=stop,
             )
 
         words = out_1[0].rearrange("p n i -> p (n i)").bitcast(I32)
         scale_rows = out_2[0].bitcast(I32)
+        out_rows = out_0.rearrange("(p r) n -> p r n", r=PACK)
 
-        def store_words(h):
-            cols = slice(h * HALF, (h + 1) * HALF)
-            nc.sync.dma_start(out=words[:, cols], in_=out_codes[:, cols].bitcast(I32))
+        def store_words(span):
+            nc.sync.dma_start(out=words[:, span[0] : span[1]], in_=out_q[0][:, span[0] : span[1]].bitcast(I32))
 
-        run(interleave_dealt, x_raw, x_q, E4M3, 2, 3, nothing, 176)
-        late_quantize(2, 0, cast(interleave, late_raw[2, 0], 88))
-        second_product(1, 1)
-        x3_grouped = new_grouped()
-        deal_pair(nc.vector.tensor_copy, x3_grouped, x_raw[3], 0, 0, P)
-        deal_pair(nc.scalar.copy, x3_grouped, x_raw[3], 1, 0, 80)
-        deal_pair(nc.vector.tensor_copy, x3_grouped, x_raw[3], 1, 80, P)
-        quantize(x3_grouped[:, : PACK * HALF], x_q[3][0][:, :HALF], x_q[3][1][:, :HALF], E4M3)
-        grouped = cast(interleave, late_raw[3, 0], 104)
-        quantize(x3_grouped[:, PACK * HALF :], x_q[3][0][:, HALF:], x_q[3][1][:, HALF:], E4M3)
-        quantize(grouped, late_q[3][0][:, :HALF], late_q[3][1][:, :HALF], E5M2)
-        multiply_half(0, x_q[3], late_q[3], True)
-        late_quantize(2, 1, cast(interleave, late_raw[2, 1], 88))
-        drain(0, 0)
+        def store_scales():
+            for q in range(4):
+                queue = nc.sync if q < 2 else nc.scalar
+                queue.dma_start(out=scale_rows[4 * q : 4 * q + 4, :], in_=out_q[1][32 * q : 32 * q + 4, :].bitcast(I32))
+
+        def nothing():
+            return None
+
+        banks = [[psum.tile([P, HALF], F32, name="sum%d_%d" % (h, r)) for r in range(PACK)] for h in range(2)]
+        result = [keep.tile([P, PACK, HALF], F32, name="result%d" % h, align_bytes=256) for h in range(2)]
+        halves = (LEFT, RIGHT)
+
+        def multiply(product, g, h):
+            stat, stat_fmt, mov, mov_fmt = ((xd_q, E5M2, w_q, E4M3), (x_q, E4M3, wd_q, E5M2))[product]
+            first = (product, g) == (0, 0)
+            last = (product, g) == (1, PASSES - 1)
+            for r in range(PACK):
+                matmul(banks[h][r][:], stat[g], stat_fmt, r, mov[g], mov_fmt, halves[h], first, last)
+
+        def whole_pass(product, g):
+            def go():
+                for h in range(2):
+                    multiply(product, g, h)
+
+            return go
+
+        def drain(copy, h, r):
+            copy(out=result[h][:, r, :], in_=banks[h][r][:])
+
+        def store_result(h, r0, r1):
+            nc.sync.dma_start(out=out_rows[:, r0:r1, h * HALF : (h + 1) * HALF], in_=result[h][:, r0:r1, :])
+
+        xd_raw = load_passes("xd_raw", xd, 0, 4)
+        w_raw = load_passes("w_raw01", w, 0, 2) + load_passes("w_raw23", w, 2, 4)
+        x_raw = load_passes("x_raw01", x, 0, 2) + load_passes("x_raw2", x, 2, 3) + load_passes("x_raw3", x, 3, 4)
+        wd_raw = [load_passes("wd_raw%d" % g, wd, g, g + 1)[0] for g in range(2)]
+        half_raw = {(1, h): wd_raw[1][:, :, span[0] : span[1]] for h, span in enumerate(halves)}
+        for h, span in enumerate(halves):
+            for g in (2, 3):
+                half_raw.setdefault((g, h), load_columns("wd_raw%d_%d" % (g, h), wd, g, span))
+        half_grouped = {key: own_grouped("wd_grouped%d_%d" % key, HALF) for key in half_raw}
+        out_grouped = [own_grouped("out_grouped%d" % h, HALF) for h in range(2)]
+
+        x_jobs = [(interleave_dealt, x_raw[g], x_q[g], E4M3, nothing) for g in range(PASSES)]
+        xd_jobs = [(interleave_dealt, xd_raw[g], xd_q[g], E5M2, nothing) for g in range(PASSES)]
+        w_jobs = [(interleave, w_raw[g], w_q[g], E4M3, whole_pass(0, g)) for g in range(PASSES)]
+        run(xd_jobs, 240)
+        run(w_jobs[:2], 240)
+        run(w_jobs[2:3], 176)
+        run(x_jobs[:3] + w_jobs[3:] + x_jobs[3:], 240)
+        run([(interleave, wd_raw[0], wd_q[0], E5M2, whole_pass(1, 0))], 176)
+
+        def cast_out(copy, h, c0, c1):
+            interleave(copy, out_grouped[h], result[h][:], c0, c1)
+
+        def cast_half(g, h, scalar_columns):
+            shared(interleave, half_grouped[g, h], half_raw[g, h], scalar_columns)
+
+        def finish_half(g, h):
+            quantize(half_grouped[g, h][:], wd_q[g], halves[h], E5M2)
+            multiply(1, g, h)
+
+        def quantize_out(h, c0, c1):
+            quantize(out_grouped[h][:, PACK * c0 : PACK * c1], out_q, (h * HALF + c0, h * HALF + c1), E4M3)
+
+        def quantize_half(g, h):
+            quantize(half_grouped[g, h][:], wd_q[g], halves[h], E5M2)
+
+        def cast_in(copy, g, h, c0, c1):
+            interleave(copy, half_grouped[g, h], half_raw[g, h], c0, c1)
+
+        cast_half(1, 0, 104)
+        cast_half(1, 1, 104)
+        finish_half(1, 0)
+        cast_half(2, 0, 104)
+        quantize_half(1, 1)
+        finish_half(2, 0)
+        cast_half(3, 0, 104)
+        finish_half(3, 0)
+        multiply(1, 1, 1)
+        cast_half(2, 1, 88)
+        finish_half(2, 1)
+        drain(on_scalar, 0, 0)
         store_result(0, 0, 1)
-        grouped = cast(interleave, late_raw[3, 1], 88)
-        drain(0, 1, nc.vector.tensor_copy)
+        cast_half(3, 1, 88)
+        drain(on_vector, 0, 1)
         store_result(0, 1, 2)
-        late_quantize(3, 1, grouped)
-        drain(0, 2)
+        finish_half(3, 1)
+        drain(on_scalar, 0, 2)
         store_result(0, 2, 3)
-        drain(0, 3)
+        drain(on_scalar, 0, 3)
         store_result(0, 3, 4)
-        left_grouped = cast(interleave, result[0][:], 88)
-        drain(1, 0)
-        quantize(left_grouped, out_codes[:, :HALF], out_scales[:, :HALF], E4M3)
-        store_words(0)
-        drain(1, 1)
+        cast_out(on_scalar, 0, 0, 64)
+        cast_out(on_vector, 0, 64, HALF)
+        drain(on_scalar, 1, 0)
+        drain(on_vector, 1, 1)
         store_result(1, 0, 2)
-        drain(1, 2, nc.vector.tensor_copy)
-        quarter = HALF // 2
-        for c in range(2):
-            nc.scalar.copy(out=result[1][:, 3, c * quarter : (c + 1) * quarter], in_=banks[1][3][:, HALF + c * quarter : HALF + (c + 1) * quarter])
+        drain(on_scalar, 1, 2)
+        drain(on_vector, 1, 3)
         store_result(1, 2, 4)
-        grouped = new_grouped()
-        interleave(nc.vector.tensor_copy, grouped, result[1][:], 0, quarter)
-        interleave(nc.scalar.copy, grouped, result[1][:], quarter, quarter + 64)
-        interleave(nc.vector.tensor_copy, grouped, result[1][:], quarter + 64, HALF)
-        for c in range(2):
-            cols = slice(HALF + c * quarter, HALF + (c + 1) * quarter)
-            quantize(grouped[:, c * PACK * quarter : (c + 1) * PACK * quarter], out_codes[:, cols], out_scales[:, cols], E4M3)
-        store_words(1)
-        for q in range(4):
-            queue = nc.sync if q < 2 else nc.scalar
-            queue.dma_start(out=scale_rows[4 * q : 4 * q + 4, :], in_=out_scales[32 * q : 32 * q + 4, :].bitcast(I32))
+        quantize_out(0, 0, HALF)
+        store_words(LEFT)
+        for c0, scalar_columns in ((0, 72), (QUARTER, 56)):
+            cast_out(on_scalar, 1, c0, c0 + scalar_columns)
+            cast_out(on_vector, 1, c0 + scalar_columns, c0 + QUARTER)
+        quantize_out(1, 0, QUARTER)
+        quantize_out(1, QUARTER, HALF)
+        store_words(RIGHT)
+        store_scales()

@@ -155,8 +155,9 @@ def tile_mix_jvp_tm_pl_none_kernel(tc, w, xd, wd, x, out_0, out_1, out_2):
             nc.sync.dma_start(out=out_rows[:, r0:r1, h * HALF : (h + 1) * HALF], in_=result[h][:, r0:r1, :])
 
         xd_raw = load_passes("xd_raw", xd, 0, 4)
-        w_raw = load_passes("w_raw01", w, 0, 2) + load_passes("w_raw23", w, 2, 4)
+        w_raw = load_passes("w_raw012", w, 0, 3)
         x_raw = load_passes("x_raw01", x, 0, 2) + load_passes("x_raw2", x, 2, 3) + load_passes("x_raw3", x, 3, 4)
+        w_raw = w_raw + load_passes("w_raw3", w, 3, 4)
         wd_raw = [load_passes("wd_raw%d" % g, wd, g, g + 1)[0] for g in range(2)]
         half_raw = {(1, h): wd_raw[1][:, :, span[0] : span[1]] for h, span in enumerate(halves)}
         for h, span in enumerate(halves):
@@ -169,10 +170,10 @@ def tile_mix_jvp_tm_pl_none_kernel(tc, w, xd, wd, x, out_0, out_1, out_2):
         xd_jobs = [(interleave_dealt, xd_raw[g], xd_q[g], E5M2, nothing) for g in range(PASSES)]
         w_jobs = [(interleave, w_raw[g], w_q[g], E4M3, whole_pass(0, g)) for g in range(PASSES)]
         run(xd_jobs, 240)
-        run(w_jobs[:2], 240)
-        run(w_jobs[2:3], 176)
-        run(x_jobs[:3] + w_jobs[3:] + x_jobs[3:], 240)
-        run([(interleave, wd_raw[0], wd_q[0], E5M2, whole_pass(1, 0))], 176)
+        run(w_jobs[:3], 240)
+        run(x_jobs, 240)
+        run(w_jobs[3:], 208)
+        run([(interleave, wd_raw[0], wd_q[0], E5M2, whole_pass(1, 0))], 208)
 
         def cast_out(copy, h, c0, c1):
             interleave(copy, out_grouped[h], result[h][:], c0, c1)
@@ -193,13 +194,15 @@ def tile_mix_jvp_tm_pl_none_kernel(tc, w, xd, wd, x, out_0, out_1, out_2):
         def cast_in(copy, g, h, c0, c1):
             interleave(copy, half_grouped[g, h], half_raw[g, h], c0, c1)
 
-        cast_half(1, 0, 104)
-        cast_half(1, 1, 104)
+        cast_half(1, 0, 120)
+        cast_in(on_scalar, 1, 1, 0, 128)
+        cast_in(on_vector, 1, 1, 128, 192)
         finish_half(1, 0)
-        cast_half(2, 0, 104)
-        quantize_half(1, 1)
+        cast_half(2, 0, 120)
+        cast_in(on_vector, 1, 1, 192, HALF)
         finish_half(2, 0)
-        cast_half(3, 0, 104)
+        cast_half(3, 0, 120)
+        quantize_half(1, 1)
         finish_half(3, 0)
         multiply(1, 1, 1)
         cast_half(2, 1, 88)
@@ -214,13 +217,13 @@ def tile_mix_jvp_tm_pl_none_kernel(tc, w, xd, wd, x, out_0, out_1, out_2):
         store_result(0, 2, 3)
         drain(on_scalar, 0, 3)
         store_result(0, 3, 4)
-        cast_out(on_scalar, 0, 0, 64)
-        cast_out(on_vector, 0, 64, HALF)
-        drain(on_scalar, 1, 0)
-        drain(on_vector, 1, 1)
+        cast_out(on_scalar, 0, 0, 88)
+        cast_out(on_vector, 0, 88, HALF)
+        drain(on_vector, 1, 0)
+        drain(on_scalar, 1, 1)
         store_result(1, 0, 2)
-        drain(on_scalar, 1, 2)
-        drain(on_vector, 1, 3)
+        drain(on_vector, 1, 2)
+        drain(on_scalar, 1, 3)
         store_result(1, 2, 4)
         quantize_out(0, 0, HALF)
         store_words(LEFT)

@@ -156,12 +156,12 @@ def tile_mix_jvp_tm_pl_none_kernel(tc, w, xd, wd, x, out_0, out_1, out_2):
 
         xd_raw = load_passes("xd_raw", xd, 0, 4)
         w_raw = load_passes("w_raw012", w, 0, 3)
-        x_raw = load_passes("x_raw01", x, 0, 2) + load_passes("x_raw2", x, 2, 3) + load_passes("x_raw3", x, 3, 4)
+        x_raw = load_passes("x_raw01", x, 0, 2) + load_passes("x_raw23", x, 2, 4)
         w_raw = w_raw + load_passes("w_raw3", w, 3, 4)
-        wd_raw = [load_passes("wd_raw%d" % g, wd, g, g + 1)[0] for g in range(2)]
-        half_raw = {(1, h): wd_raw[1][:, :, span[0] : span[1]] for h, span in enumerate(halves)}
+        wd_raw0 = load_passes("wd_raw0", wd, 0, 1)[0]
+        half_raw = {(0, h): wd_raw0[:, :, span[0] : span[1]] for h, span in enumerate(halves)}
         for h, span in enumerate(halves):
-            for g in (2, 3):
+            for g in range(1, PASSES):
                 half_raw.setdefault((g, h), load_columns("wd_raw%d_%d" % (g, h), wd, g, span))
         half_grouped = {key: own_grouped("wd_grouped%d_%d" % key, HALF) for key in half_raw}
         out_grouped = [own_grouped("out_grouped%d" % h, HALF) for h in range(2)]
@@ -171,9 +171,8 @@ def tile_mix_jvp_tm_pl_none_kernel(tc, w, xd, wd, x, out_0, out_1, out_2):
         w_jobs = [(interleave, w_raw[g], w_q[g], E4M3, whole_pass(0, g)) for g in range(PASSES)]
         run(xd_jobs, 240)
         run(w_jobs[:3], 240)
-        run(x_jobs, 240)
-        run(w_jobs[3:], 208)
-        run([(interleave, wd_raw[0], wd_q[0], E5M2, whole_pass(1, 0))], 208)
+        run(x_jobs[:2], 240)
+        run(x_jobs[2:] + w_jobs[3:], 240)
 
         def cast_out(copy, h, c0, c1):
             interleave(copy, out_grouped[h], result[h][:], c0, c1)
@@ -194,31 +193,38 @@ def tile_mix_jvp_tm_pl_none_kernel(tc, w, xd, wd, x, out_0, out_1, out_2):
         def cast_in(copy, g, h, c0, c1):
             interleave(copy, half_grouped[g, h], half_raw[g, h], c0, c1)
 
-        cast_half(1, 0, 120)
-        cast_in(on_scalar, 1, 1, 0, 128)
-        cast_in(on_vector, 1, 1, 128, 192)
+        cast_half(0, 0, 104)
+        cast_in(on_scalar, 0, 1, 0, 128)
+        cast_in(on_vector, 0, 1, 128, 192)
+        finish_half(0, 0)
+        cast_half(1, 0, 104)
+        cast_in(on_vector, 0, 1, 192, HALF)
         finish_half(1, 0)
-        cast_half(2, 0, 120)
-        cast_in(on_vector, 1, 1, 192, HALF)
+        cast_half(2, 0, 104)
+        quantize_half(0, 1)
         finish_half(2, 0)
-        cast_half(3, 0, 120)
-        quantize_half(1, 1)
+        multiply(1, 0, 1)
+        cast_half(3, 0, 96)
         finish_half(3, 0)
-        multiply(1, 1, 1)
+        cast_half(1, 1, 88)
+        finish_half(1, 1)
+        drain(on_scalar, 0, 0)
+        drain(on_scalar, 0, 1)
+        store_result(0, 0, 2)
         cast_half(2, 1, 88)
         finish_half(2, 1)
-        drain(on_scalar, 0, 0)
-        store_result(0, 0, 1)
-        cast_half(3, 1, 88)
-        drain(on_vector, 0, 1)
-        store_result(0, 1, 2)
-        finish_half(3, 1)
         drain(on_scalar, 0, 2)
-        store_result(0, 2, 3)
         drain(on_scalar, 0, 3)
-        store_result(0, 3, 4)
-        cast_out(on_scalar, 0, 0, 88)
-        cast_out(on_vector, 0, 88, HALF)
+        store_result(0, 2, 4)
+        cast_in(on_scalar, 3, 1, 0, 48)
+        cast_in(on_vector, 3, 1, 48, QUARTER)
+        cast_in(on_scalar, 3, 1, QUARTER, QUARTER + 40)
+        cast_in(on_vector, 3, 1, QUARTER + 40, HALF)
+        for c0 in (0, QUARTER):
+            quantize(half_grouped[3, 1][:, PACK * c0 : PACK * (c0 + QUARTER)], wd_q[3], (HALF + c0, HALF + c0 + QUARTER), E5M2)
+        multiply(1, 3, 1)
+        cast_out(on_scalar, 0, 0, 160)
+        cast_out(on_vector, 0, 160, HALF)
         drain(on_vector, 1, 0)
         drain(on_scalar, 1, 1)
         store_result(1, 0, 2)
@@ -227,9 +233,9 @@ def tile_mix_jvp_tm_pl_none_kernel(tc, w, xd, wd, x, out_0, out_1, out_2):
         store_result(1, 2, 4)
         quantize_out(0, 0, HALF)
         store_words(LEFT)
-        for c0, scalar_columns in ((0, 72), (QUARTER, 56)):
-            cast_out(on_scalar, 1, c0, c0 + scalar_columns)
-            cast_out(on_vector, 1, c0 + scalar_columns, c0 + QUARTER)
+        for c0 in (0, QUARTER):
+            cast_out(on_scalar, 1, c0, c0 + 56)
+            cast_out(on_vector, 1, c0 + 56, c0 + QUARTER)
         quantize_out(1, 0, QUARTER)
         quantize_out(1, QUARTER, HALF)
         store_words(RIGHT)

@@ -155,9 +155,9 @@ def tile_mix_jvp_tm_pl_none_kernel(tc, w, xd, wd, x, out_0, out_1, out_2):
             nc.sync.dma_start(out=out_rows[:, r0:r1, h * HALF : (h + 1) * HALF], in_=result[h][:, r0:r1, :])
 
         xd_raw = load_passes("xd_raw", xd, 0, 4)
-        w_raw = load_passes("w_raw012", w, 0, 3)
-        x_raw = load_passes("x_raw01", x, 0, 2) + load_passes("x_raw23", x, 2, 4)
-        w_raw = w_raw + load_passes("w_raw3", w, 3, 4)
+        x_raw = load_passes("x_raw012", x, 0, 3)
+        w_raw = load_passes("w_raw01", w, 0, 2) + load_passes("w_raw23", w, 2, 4)
+        x_raw = x_raw + load_passes("x_raw3", x, 3, 4)
         wd_raw0 = load_passes("wd_raw0", wd, 0, 1)[0]
         half_raw = {(0, h): wd_raw0[:, :, span[0] : span[1]] for h, span in enumerate(halves)}
         for h, span in enumerate(halves):
@@ -170,9 +170,9 @@ def tile_mix_jvp_tm_pl_none_kernel(tc, w, xd, wd, x, out_0, out_1, out_2):
         xd_jobs = [(interleave_dealt, xd_raw[g], xd_q[g], E5M2, nothing) for g in range(PASSES)]
         w_jobs = [(interleave, w_raw[g], w_q[g], E4M3, whole_pass(0, g)) for g in range(PASSES)]
         run(xd_jobs, 240)
-        run(w_jobs[:3], 240)
-        run(x_jobs[:2], 240)
-        run(x_jobs[2:] + w_jobs[3:], 240)
+        run(x_jobs[:3], 240)
+        run(w_jobs[:2], 240)
+        run(w_jobs[2:] + x_jobs[3:], 240)
 
         def cast_out(copy, h, c0, c1):
             interleave(copy, out_grouped[h], result[h][:], c0, c1)
@@ -203,9 +203,9 @@ def tile_mix_jvp_tm_pl_none_kernel(tc, w, xd, wd, x, out_0, out_1, out_2):
         cast_half(2, 0, 104)
         quantize_half(0, 1)
         finish_half(2, 0)
-        multiply(1, 0, 1)
         cast_half(3, 0, 96)
         finish_half(3, 0)
+        multiply(1, 0, 1)
         cast_half(1, 1, 88)
         finish_half(1, 1)
         drain(on_scalar, 0, 0)

@@ -161,8 +161,10 @@ def tile_mix_jvp_tm_pl_none_kernel(tc, w, xd, wd, x, out_0, out_1, out_2):
         wd_raw0 = load_passes("wd_raw0", wd, 0, 1)[0]
         half_raw = {(0, h): wd_raw0[:, :, span[0] : span[1]] for h, span in enumerate(halves)}
         for h, span in enumerate(halves):
-            for g in range(1, PASSES):
+            for g in range(1, PASSES - h):
                 half_raw.setdefault((g, h), load_columns("wd_raw%d_%d" % (g, h), wd, g, span))
+        last_raw = [load_columns("wd_raw3_quarter%d" % c, wd, 3, span) for c, span in enumerate((MID, LAST))]
+        last_grouped = [own_grouped("wd_grouped3_quarter%d" % c, QUARTER) for c in range(2)]
         half_grouped = {key: own_grouped("wd_grouped%d_%d" % key, HALF) for key in half_raw}
         out_grouped = [own_grouped("out_grouped%d" % h, HALF) for h in range(2)]
 
@@ -209,22 +211,21 @@ def tile_mix_jvp_tm_pl_none_kernel(tc, w, xd, wd, x, out_0, out_1, out_2):
         cast_half(1, 1, 88)
         finish_half(1, 1)
         drain(on_scalar, 0, 0)
+        store_result(0, 0, 1)
         drain(on_scalar, 0, 1)
-        store_result(0, 0, 2)
+        store_result(0, 1, 2)
         cast_half(2, 1, 88)
+        shared(interleave, last_grouped[0], last_raw[0], 48)
         finish_half(2, 1)
         drain(on_scalar, 0, 2)
+        shared(interleave, last_grouped[1], last_raw[1], 48)
+        quantize(last_grouped[0][:], wd_q[3], MID, E5M2)
+        quantize(last_grouped[1][:], wd_q[3], LAST, E5M2)
+        multiply(1, 3, 1)
         drain(on_scalar, 0, 3)
         store_result(0, 2, 4)
-        cast_in(on_scalar, 3, 1, 0, 48)
-        cast_in(on_vector, 3, 1, 48, QUARTER)
-        cast_in(on_scalar, 3, 1, QUARTER, QUARTER + 40)
-        cast_in(on_vector, 3, 1, QUARTER + 40, HALF)
-        for c0 in (0, QUARTER):
-            quantize(half_grouped[3, 1][:, PACK * c0 : PACK * (c0 + QUARTER)], wd_q[3], (HALF + c0, HALF + c0 + QUARTER), E5M2)
-        multiply(1, 3, 1)
-        cast_out(on_scalar, 0, 0, 160)
-        cast_out(on_vector, 0, 160, HALF)
+        cast_out(on_scalar, 0, 0, QUARTER)
+        cast_out(on_vector, 0, QUARTER, HALF)
         drain(on_vector, 1, 0)
         drain(on_scalar, 1, 1)
         store_result(1, 0, 2)

@@ -141,6 +141,11 @@ def tile_mix_jvp_tm_pl_none_kernel(tc, w, xd, wd, x, out_0, out_1, out_2):
             for r in range(PACK):
                 matmul(banks[h][r][:], stat[g], stat_fmt, r, mov[g], mov_fmt, halves[h], first, last)
 
+        def multiply_last(span, last):
+            for r in range(PACK):
+                out = banks[1][r][:, span[0] - HALF : span[1] - HALF]
+                matmul(out, x_q[3], E4M3, r, wd_q[3], E5M2, span, False, last)
+
         def whole_pass(product, g):
             def go():
                 for h in range(2):
@@ -220,8 +225,9 @@ def tile_mix_jvp_tm_pl_none_kernel(tc, w, xd, wd, x, out_0, out_1, out_2):
         drain(on_scalar, 0, 2)
         shared(interleave, last_grouped[1], last_raw[1], 48)
         quantize(last_grouped[0][:], wd_q[3], MID, E5M2)
+        multiply_last(MID, False)
         quantize(last_grouped[1][:], wd_q[3], LAST, E5M2)
-        multiply(1, 3, 1)
+        multiply_last(LAST, True)
         drain(on_scalar, 0, 3)
         store_result(0, 2, 4)
         cast_out(on_scalar, 0, 0, QUARTER)

@@ -72,8 +72,8 @@ def tile_mix_jvp_tm_pl_none_kernel(tc, w, xd, wd, x, out_0, out_1, out_2):
 
         def interleave(copy, grouped, raw, c0, c1):
             copy(
-                out=grouped[:, PACK * c0 : PACK * c1].rearrange("p (c i j) -> p c j i", i=4, j=PACK),
-                in_=raw[:, :, c0:c1].rearrange("p j (c i) -> p c j i", i=4),
+                out=grouped[:, PACK * c0 : PACK * c1].rearrange("p (c i j) -> p c j i", i=2, j=PACK),
+                in_=raw[:, :, c0:c1].rearrange("p j (c i) -> p c j i", i=2),
             )
 
         def interleave_dealt(copy, grouped, raw, c0, c1):

from contextlib import ExitStack

import concourse.mybir as mybir

K, M, T = 2048, 512, 512
FLOPS = 2 * 2 * K * M * T

F32 = mybir.dt.float32
BF16 = mybir.dt.bfloat16
I32 = mybir.dt.int32
U32 = mybir.dt.uint32
U8 = mybir.dt.uint8
E4M3 = mybir.dt.float8_e4m3fn_x4
E5M2 = mybir.dt.float8_e5m2_x4

P = 128
PACK = 4
K_PASS = P * PACK
PASSES = K // K_PASS
HALF = M // 2
QUARTER = M // 4
LEFT = (0, HALF)
RIGHT = (HALF, M)
MID = (HALF, HALF + QUARTER)
LAST = (HALF + QUARTER, M)


def tile_mix_jvp_tm_pl_none_kernel(tc, w, xd, wd, x, out_0, out_1, out_2):
    nc = tc.nc
    with ExitStack() as ctx:
        keep = ctx.enter_context(tc.tile_pool(name="keep", bufs=1))
        stage = ctx.enter_context(tc.tile_pool(name="stage", bufs=6))
        psum = ctx.enter_context(tc.psum_pool(name="psum", bufs=1))
        ctx.enter_context(tc.manual_schedule())
        on_scalar = nc.scalar.copy
        on_vector = nc.vector.tensor_copy

        def load_passes(name, src, g0, g1):
            raw = keep.tile([P, g1 - g0, PACK, M], F32, name=name, align_bytes=256)
            nc.sync.dma_start(
                out=raw[:].rearrange("p g j n -> p g (j n)"),
                in_=src[g0 * K_PASS : g1 * K_PASS, :].rearrange("(g p j) n -> p g (j n)", p=P, j=PACK),
            )
            return [raw[:, g, :, :] for g in range(g1 - g0)]

        def load_columns(name, src, g, span):
            raw = keep.tile([P, PACK, span[1] - span[0]], F32, name=name, align_bytes=256)
            nc.sync.dma_start(
                out=raw[:],
                in_=src[g * K_PASS : (g + 1) * K_PASS, span[0] : span[1]].rearrange("(p j) n -> p j n", j=PACK),
            )
            return raw[:]

        def mx_tiles(name):
            codes = keep.tile([P, M], U32, name=name + "_codes", align_bytes=256)
            scales = keep.tile([P, M], U8, name=name + "_scales", align_bytes=256)
            return codes, scales

        xd_q = [mx_tiles("xd%d" % g) for g in range(PASSES)]
        w_q = [mx_tiles("w%d" % g) for g in range(PASSES)]
        x_q = [mx_tiles("x%d" % g) for g in range(PASSES)]
        wd_q = [mx_tiles("wd%d" % g) for g in range(PASSES)]
        out_q = mx_tiles("out")

        def whole_grouped():
            grouped = stage.tile([P, PACK * M], BF16, name="grouped", align_bytes=256)
            return grouped

        def own_grouped(name, width):
            grouped = keep.tile([P, PACK * width], BF16, name=name, align_bytes=256)
            return grouped

        def interleave(copy, grouped, raw, c0, c1):
            copy(
                out=grouped[:, PACK * c0 : PACK * c1].rearrange("p (c i j) -> p c j i", i=2, j=PACK),
                in_=raw[:, :, c0:c1].rearrange("p j (c i) -> p c j i", i=2),
            )

        def interleave_dealt(copy, grouped, raw, c0, c1):
            copy(
                out=grouped[:].rearrange("p (r m j) -> p m j r", r=PACK, j=PACK)[:, c0 // PACK : c1 // PACK, :, :],
                in_=raw[:, :, c0:c1].rearrange("p j (m r) -> p m j r", r=PACK),
            )

        def shared(kind, grouped, raw, scalar_columns):
            kind(on_scalar, grouped, raw, 0, scalar_columns)
            kind(on_vector, grouped, raw, scalar_columns, raw.shape[2])

        def quantize(grouped, tiles, span, fmt):
            nc.vector.quantize_mx(
                out=tiles[0][:, span[0] : span[1]].bitcast(fmt), scales=tiles[1][:, span[0] : span[1]], in_=grouped
            )

        def run(jobs, scalar_columns):
            pending = None
            for job in jobs + [None]:
                grouped = None
                if job is not None:
                    grouped = whole_grouped()
                    shared(job[0], grouped, job[1], scalar_columns)
                if pending is not None:
                    quantize(pending[0][:], pending[1][2], (0, M), pending[1][3])
                    pending[1][4]()
                pending = (grouped, job)

        def matmul(out, stat, stat_fmt, r, mov, mov_fmt, span, start, stop):
            cols = slice(r * P, (r + 1) * P)
            nc.tensor.matmul_mx(
                out=out,
                lhsT=stat[0][:, cols].bitcast(stat_fmt),
                lhsT_scale=stat[1][:, cols],
                rhs=mov[0][:, span[0] : span[1]].bitcast(mov_fmt),
                rhs_scale=mov[1][:, span[0] : span[1]],
                start=start,
                stop=stop,
            )

        words = out_1[0].rearrange("p n i -> p (n i)").bitcast(I32)
        scale_rows = out_2[0].bitcast(I32)
        out_rows = out_0.rearrange("(p r) n -> p r n", r=PACK)

        def store_words(span):
            nc.sync.dma_start(out=words[:, span[0] : span[1]], in_=out_q[0][:, span[0] : span[1]].bitcast(I32))

        def store_scales():
            for q in range(4):
                queue = nc.sync if q < 2 else nc.scalar
                queue.dma_start(out=scale_rows[4 * q : 4 * q + 4, :], in_=out_q[1][32 * q : 32 * q + 4, :].bitcast(I32))

        def nothing():
            return None

        banks = [[psum.tile([P, HALF], F32, name="sum%d_%d" % (h, r)) for r in range(PACK)] for h in range(2)]
        result = [keep.tile([P, PACK, HALF], F32, name="result%d" % h, align_bytes=256) for h in range(2)]
        halves = (LEFT, RIGHT)

        def multiply(product, g, h):
            stat, stat_fmt, mov, mov_fmt = ((xd_q, E5M2, w_q, E4M3), (x_q, E4M3, wd_q, E5M2))[product]
            first = (product, g) == (0, 0)
            last = (product, g) == (1, PASSES - 1)
            for r in range(PACK):
                matmul(banks[h][r][:], stat[g], stat_fmt, r, mov[g], mov_fmt, halves[h], first, last)

        def multiply_last(span, last):
            for r in range(PACK):
                out = banks[1][r][:, span[0] - HALF : span[1] - HALF]
                matmul(out, x_q[3], E4M3, r, wd_q[3], E5M2, span, False, last)

        def whole_pass(product, g):
            def go():
                for h in range(2):
                    multiply(product, g, h)

            return go

        def drain(copy, h, r):
            copy(out=result[h][:, r, :], in_=banks[h][r][:])

        def store_result(h, r0, r1):
            nc.sync.dma_start(out=out_rows[:, r0:r1, h * HALF : (h + 1) * HALF], in_=result[h][:, r0:r1, :])

        xd_raw = load_passes("xd_raw", xd, 0, 4)
        x_raw = load_passes("x_raw012", x, 0, 3)
        w_raw = load_passes("w_raw01", w, 0, 2) + load_passes("w_raw23", w, 2, 4)
        x_raw = x_raw + load_passes("x_raw3", x, 3, 4)
        wd_raw0 = load_passes("wd_raw0", wd, 0, 1)[0]
        half_raw = {(0, h): wd_raw0[:, :, span[0] : span[1]] for h, span in enumerate(halves)}
        for h, span in enumerate(halves):
            for g in range(1, PASSES - h):
                half_raw.setdefault((g, h), load_columns("wd_raw%d_%d" % (g, h), wd, g, span))
        last_raw = [load_columns("wd_raw3_quarter%d" % c, wd, 3, span) for c, span in enumerate((MID, LAST))]
        last_grouped = [own_grouped("wd_grouped3_quarter%d" % c, QUARTER) for c in range(2)]
        half_grouped = {key: own_grouped("wd_grouped%d_%d" % key, HALF) for key in half_raw}
        out_grouped = [own_grouped("out_grouped%d" % h, HALF) for h in range(2)]

        x_jobs = [(interleave_dealt, x_raw[g], x_q[g], E4M3, nothing) for g in range(PASSES)]
        xd_jobs = [(interleave_dealt, xd_raw[g], xd_q[g], E5M2, nothing) for g in range(PASSES)]
        w_jobs = [(interleave, w_raw[g], w_q[g], E4M3, whole_pass(0, g)) for g in range(PASSES)]
        run(xd_jobs, 240)
        run(x_jobs[:3], 240)
        run(w_jobs[:2], 240)
        run(w_jobs[2:] + x_jobs[3:], 240)

        def cast_out(copy, h, c0, c1):
            interleave(copy, out_grouped[h], result[h][:], c0, c1)

        def cast_half(g, h, scalar_columns):
            shared(interleave, half_grouped[g, h], half_raw[g, h], scalar_columns)

        def finish_half(g, h):
            quantize(half_grouped[g, h][:], wd_q[g], halves[h], E5M2)
            multiply(1, g, h)

        def quantize_out(h, c0, c1):
            quantize(out_grouped[h][:, PACK * c0 : PACK * c1], out_q, (h * HALF + c0, h * HALF + c1), E4M3)

        def quantize_half(g, h):
            quantize(half_grouped[g, h][:], wd_q[g], halves[h], E5M2)

        def cast_in(copy, g, h, c0, c1):
            interleave(copy, half_grouped[g, h], half_raw[g, h], c0, c1)

        cast_half(0, 0, 104)
        cast_in(on_scalar, 0, 1, 0, 128)
        cast_in(on_vector, 0, 1, 128, 192)
        finish_half(0, 0)
        cast_half(1, 0, 104)
        cast_in(on_vector, 0, 1, 192, HALF)
        finish_half(1, 0)
        cast_half(2, 0, 104)
        quantize_half(0, 1)
        finish_half(2, 0)
        cast_half(3, 0, 96)
        finish_half(3, 0)
        multiply(1, 0, 1)
        cast_half(1, 1, 88)
        finish_half(1, 1)
        drain(on_scalar, 0, 0)
        store_result(0, 0, 1)
        drain(on_scalar, 0, 1)
        store_result(0, 1, 2)
        cast_half(2, 1, 88)
        shared(interleave, last_grouped[0], last_raw[0], 48)
        finish_half(2, 1)
        drain(on_scalar, 0, 2)
        shared(interleave, last_grouped[1], last_raw[1], 48)
        quantize(last_grouped[0][:], wd_q[3], MID, E5M2)
        multiply_last(MID, False)
        quantize(last_grouped[1][:], wd_q[3], LAST, E5M2)
        multiply_last(LAST, True)
        drain(on_scalar, 0, 3)
        store_result(0, 2, 4)
        cast_out(on_scalar, 0, 0, QUARTER)
        cast_out(on_vector, 0, QUARTER, HALF)
        drain(on_vector, 1, 0)
        drain(on_scalar, 1, 1)
        store_result(1, 0, 2)
        drain(on_vector, 1, 2)
        drain(on_scalar, 1, 3)
        store_result(1, 2, 4)
        quantize_out(0, 0, HALF)
        store_words(LEFT)
        for c0 in (0, QUARTER):
            cast_out(on_scalar, 1, c0, c0 + 56)
            cast_out(on_vector, 1, c0 + 56, c0 + QUARTER)
        quantize_out(1, 0, QUARTER)
        quantize_out(1, QUARTER, HALF)
        store_words(RIGHT)
        store_scales()
